import numpy as np
import ml_dtypes


def mxq(x, axis, fmt="e4m3"):
    dtype, down = {"e4m3": (ml_dtypes.float8_e4m3fn, 7), "e5m2": (ml_dtypes.float8_e5m2, 14)}[fmt]
    v = np.moveaxis(np.asarray(x, np.float32).astype(ml_dtypes.bfloat16).astype(np.float64), axis, -1)
    blocks = v.reshape(v.shape[:-1] + (-1, 32))
    amax = np.abs(blocks).max(-1, keepdims=True)
    byte = np.maximum(np.where(amax > 0, np.frexp(amax)[1] - 1 + 127, 0) - down, 1)
    scale = np.exp2(byte - 127.0)
    codes = (blocks / scale).astype(np.float32).astype(dtype).astype(np.float64)
    return np.moveaxis((codes * scale).reshape(v.shape), -1, axis)


WIDE = False


def mx_kscale(k):
    if not WIDE:
        return np.ones(k)
    levels = np.array([10, -10, 5, -5, 0])
    if k % 512:
        return np.exp2(np.random.permutation(np.resize(levels, k // 32))).repeat(32)
    a = np.empty((k // 512, 16))
    for p in range(k // 512):
        a[p, :8] = np.random.permutation(np.resize(levels, 8))
        for g in range(8):
            far = levels[np.abs(levels - a[p, g]) >= 10]
            a[p, g + 8] = far[np.random.randint(len(far))]
    return np.exp2(a.ravel()).repeat(32)


def f64(x):
    return np.asarray(x).astype(np.float64)


def striped(idx):
    return np.tile(idx.reshape(-1, 16).T, (8, 1)).astype(np.uint16)


def unstriped(offs):
    return offs[:16].T.reshape(-1).astype(np.int64)


def pack_weight(w):
    k, n = w.shape
    w = f64(np.asarray(w, np.float32).astype(ml_dtypes.bfloat16)).reshape(k // 32, 32, n)
    amax = np.abs(w).max(1)
    byte = np.clip(np.where(amax > 0, np.frexp(amax)[1] - 1 + 127 - 7, 1), 1, 254)
    scaled = (w * np.exp2(127.0 - byte)[:, None, :]).reshape(k, n).astype(np.float32)
    words = np.ascontiguousarray(scaled.reshape(k // 512, 128, 4, n).transpose(0, 1, 3, 2)).astype(ml_dtypes.float8_e4m3fn).view(np.uint8)
    return words, np.ascontiguousarray(byte.astype(np.uint8).reshape(k // 512, 16, n))


def unpack_weight(words, scales):
    g, p, n, _ = words.shape
    vals = np.ascontiguousarray(words).view(ml_dtypes.float8_e4m3fn).astype(np.float64) * np.repeat(np.exp2(scales.astype(np.float64) - 127.0), 8, axis=1)[..., None]
    return vals.transpose(0, 1, 3, 2).reshape(g * 512, n)


def sigmoid(v):
    return 1.0 / (1.0 + np.exp(-np.maximum(v, -700.0)))


K, T, S, D, N, H = 1024, 2048, 512, 4, 128, 512


def setup_inputs():
    n = np.random.standard_normal
    s = mx_kscale(K)[:, None]
    u = mx_kscale(H)
    packed_xT = pack_weight(n((K, T)) * s)
    return {
        "x_words": packed_xT[0],
        "x_scales": packed_xT[1],
        "w1": (n((K, H)) / np.sqrt(K) / s).astype(np.float32),
        "w2": (n((K, H)) / np.sqrt(K) / s).astype(np.float32),
        "den": (np.random.uniform(2.5, 3.5, (H, S))).astype(np.float32),
        "unit": (np.random.uniform(0.6, 1.4, (H, 1)) * u[:, None]).astype(np.float32),
        "w3": (n((H, N)) / np.sqrt(H) / u[:, None]).astype(np.float32),
        "offs": striped(np.random.permutation(T)[:S]),
        "shuf": striped(np.random.permutation(S)),
    }


def reference(x_words, x_scales, w1, w2, den, unit, w3, offs, shuf):
    xq = unpack_weight(x_words, x_scales)[:, unstriped(offs)]
    y = mxq(f64(w1), 0, "e4m3").T @ xq
    rew = sigmoid(y)
    rs = rew.reshape(len(rew), -1, D).sum(axis=2)
    base = (np.repeat(rs, D, axis=1) - rew) / f64(den)
    adv = rew - base
    yl = mxq(f64(w2), 0, "e4m3").T @ xq
    pgz = adv * yl
    hid = f64(unit) * (pgz + adv[:, unstriped(shuf)])
    return mxq(f64(w3), 0, "e4m3").T @ mxq(hid, 0, "e4m3")

@@ -1,0 +1,253 @@
+from contextlib import ExitStack
+
+import concourse.mybir as mybir
+from concourse.masks import make_identity
+
+K, T, S, D, N, H = 1024, 2048, 512, 4, 128, 512
+FLOPS = 2 * K * H * S * 2 + 2 * H * N * S
+
+F32 = mybir.dt.float32
+BF16 = mybir.dt.bfloat16
+I32 = mybir.dt.int32
+U32 = mybir.dt.uint32
+U16 = mybir.dt.uint16
+U8 = mybir.dt.uint8
+FP8X4 = mybir.dt.float8_e4m3fn_x4
+ACT = mybir.ActivationFunctionType
+ALU = mybir.AluOpType
+
+P = 128
+PACK = 4
+PASSES = K // (P * PACK)
+V = S // D
+CHUNKS = (256, 128, 128)
+
+
+def tile_picked_yrloov_pg_p_kernel(
+    tc, x_words, x_scales, w1, w2, den, unit, w3, offs, shuf, out
+):
+    nc = tc.nc
+    with ExitStack() as ctx:
+        keep = ctx.enter_context(tc.tile_pool(name="keep", bufs=1))
+        psum = ctx.enter_context(tc.psum_pool(name="psum", bufs=1))
+
+        def sbuf(name, shape, dtype):
+            return keep.tile(shape, dtype, name=name, align_bytes=64)
+
+        den_rows = den.rearrange("(p t) j -> p t j", t=PACK)
+        den_sb = [sbuf(f"den{h}", [P, 2, S], F32) for h in range(2)]
+        for h in range(2):
+            nc.sync.dma_start(out=den_sb[h][:], in_=den_rows[:, 2 * h : 2 * h + 2, :])
+        offs_sb = keep.tile([P, S // 16], U16, name="offs_sb")
+        nc.sync.dma_start(offs_sb[:], offs)
+
+        scale_table = sbuf("scale_table", [P, T], U8)
+        nc.vector.memset(scale_table[:].bitcast(I32), 0)
+        for q in range(4):
+            nc.scalar.dma_start(
+                out=scale_table[32 * q : 32 * q + 4 * PASSES, :].bitcast(I32),
+                in_=x_scales[:, 4 * q : 4 * q + 4, :].bitcast(I32),
+            )
+        unit_sb = sbuf("unit_sb", [P, PACK], F32)
+        nc.scalar.dma_start(out=unit_sb[:], in_=unit.rearrange("(p t) o -> p (t o)", t=PACK))
+        ident = sbuf("ident", [P, P], F32)
+        make_identity(nc, ident[:])
+
+        word_table = [sbuf(f"word_table{o}", [P, T], I32) for o in range(PASSES)]
+
+        def load_words(o):
+            nc.sync.dma_start(out=word_table[o][:], in_=x_words[o].rearrange("p n t -> p (n t)").bitcast(I32))
+
+        def load_rows(name, w, o, cols):
+            raw = sbuf(name, [P, PACK, cols.stop - cols.start], F32)
+            rows = w[o * P * PACK : (o + 1) * P * PACK, :].rearrange("(p j) c -> p j c", j=PACK)
+            nc.sync.dma_start(out=raw[:], in_=rows[:, :, cols])
+            return raw
+
+        halves = [slice(h * H // 2, (h + 1) * H // 2) for h in range(2)]
+        w1raw = {}
+        load_words(0)
+        w1raw[0, 0] = load_rows("w1raw00", w1, 0, halves[0])
+        load_words(1)
+        for h, o in ((0, 1), (1, 0), (1, 1)):
+            w1raw[h, o] = load_rows(f"w1raw{h}{o}", w1, o, halves[h])
+        w2raw = [load_rows(f"w2raw{o}", w2, o, slice(0, H)) for o in range(PASSES)]
+        w3raw = load_rows("w3raw", w3, 0, slice(0, N))
+        shuf_sb = keep.tile([P, S // 16], U16, name="shuf_sb")
+        nc.sync.dma_start(shuf_sb[:], shuf)
+
+        root = [sbuf(f"root{t}", [P, S], F32) for t in range(PACK)]
+        rabs = [sbuf(f"rabs{t}", [P, S], F32) for t in range(PACK)]
+        sign = [sbuf(f"sign{t}", [P, S], F32) for t in range(PACK)]
+        rden = [sbuf(f"rden{t}", [P, S], F32) for t in range(PACK)]
+        for t in range(PACK):
+            den_t = den_sb[t // 2][:, t % 2, :]
+            nc.scalar.activation(root[t][:], den_t, ACT.Abs_reciprocal_sqrt)
+            nc.scalar.activation(rabs[t][:], root[t][:], ACT.Square)
+            nc.scalar.activation(sign[t][:], den_t, ACT.Sign)
+        warm = sbuf("warm", [P, 1], F32)
+        nc.scalar.activation(warm[:], root[PACK - 1][:, 0:1], ACT.Sigmoid)
+
+        def signed_reciprocal(t):
+            nc.vector.tensor_tensor(rden[t][:], rabs[t][:], sign[t][:], ALU.mult)
+
+        signed_reciprocal(0)
+
+        picked = [sbuf(f"picked{o}", [P, S], U32) for o in range(PASSES)]
+        dealt = [sbuf(f"dealt{o}", [P, D, V], U32) for o in range(PASSES)]
+        picked_s = sbuf("picked_s", [P, S], U8)
+        dealt_s = sbuf("dealt_s", [P, D, V], U8)
+
+        def deal(dst, src):
+            nc.vector.tensor_copy(dst[:].rearrange("p d v -> p v d"), src[:].rearrange("p (v d) -> p v d", d=D))
+
+        def pick_words(o):
+            nc.vector.tensor_copy(picked[o][:], word_table[o][:].bitcast(U32).indirect(offs_sb[:]))
+            deal(dealt[o], picked[o])
+
+        def cast_dealt(engine_copy, grouped, raw, m0, src_m):
+            width = src_m.stop - src_m.start
+            dst = grouped[:].rearrange("p t m j -> p m j t")[:, m0 : m0 + width]
+            src = raw[:].rearrange("p j (m t) -> p m j t", t=PACK)[:, src_m]
+            engine_copy(dst, src)
+
+        def quantize(words, scales, values):
+            nc.vector.quantize_mx(out=words.bitcast(FP8X4), scales=scales, in_=values)
+
+        def interleave(engine_copy, dst, src):
+            engine_copy(dst[:].rearrange("p (c i) t -> p c t i", i=4), src[:].rearrange("p t (c i) -> p c t i", i=4))
+
+        def bank(b, name, shape):
+            return psum.tile(shape, F32, name=name, tag=f"bank{b}")
+
+        w1q, w1s = {}, {}
+
+        def prepare_w1(h, o, engine_copy):
+            grouped = sbuf(f"w1g{h}{o}", [P, H // 2, PACK], BF16)
+            interleave(engine_copy, grouped, w1raw[h, o])
+            w1q[h, o] = sbuf(f"w1q{h}{o}", [P, H // 2], U32)
+            w1s[h, o] = sbuf(f"w1s{h}{o}", [P, H // 2], U8)
+            quantize(w1q[h, o][:], w1s[h, o][:], grouped[:].rearrange("p n j -> p (n j)"))
+
+        rew_t = [sbuf(f"rew_t{d}", [P, PACK, P], F32) for d in range(D)]
+
+        def rewards(h):
+            logits = [bank(D * h + d, f"logits{h}{d}", [P, H // 2]) for d in range(D)]
+            for o in range(PASSES):
+                for d in range(D):
+                    nc.tensor.matmul_mx(
+                        out=logits[d][:],
+                        lhsT=dealt[o][:, d, :].bitcast(FP8X4),
+                        lhsT_scale=dealt_s[4 * o :, d, :],
+                        rhs=w1q[h, o][:].bitcast(FP8X4),
+                        rhs_scale=w1s[h, o][:],
+                        start=(o == 0),
+                        stop=(o == PASSES - 1),
+                    )
+            for d in range(D):
+                nc.scalar.activation(
+                    rew_t[d][:, :, 64 * h : 64 * h + 64], logits[d][:].rearrange("p (m t) -> p t m", t=PACK), ACT.Sigmoid
+                )
+
+        pick_words(0)
+        nc.vector.tensor_copy(picked_s[:], scale_table[:].indirect(offs_sb[:]))
+        deal(dealt_s, picked_s)
+        prepare_w1(0, 0, nc.vector.tensor_copy)
+        pick_words(1)
+        prepare_w1(0, 1, nc.vector.tensor_copy)
+        prepare_w1(1, 0, nc.scalar.copy)
+        rewards(0)
+        prepare_w1(1, 1, nc.vector.tensor_copy)
+        rewards(1)
+        for t in range(1, PACK):
+            signed_reciprocal(t)
+
+        w2g = [sbuf(f"w2g{o}", [P, PACK, P, PACK], BF16) for o in range(PASSES)]
+        w2q = [sbuf(f"w2q{o}", [P, H], U32) for o in range(PASSES)]
+        w2s = [sbuf(f"w2s{o}", [P, H], U8) for o in range(PASSES)]
+        for o in range(PASSES):
+            for m0 in range(0, P, 32):
+                engine_copy = nc.vector.tensor_copy if (o == 0 and m0 < 64) else nc.scalar.copy
+                cast_dealt(engine_copy, w2g[o], w2raw[o], m0, slice(m0, m0 + 32))
+            quantize(w2q[o][:], w2s[o][:], w2g[o][:].rearrange("p t m j -> p (t m j)"))
+
+        base = [sbuf(f"base{t}", [P, S], F32) for t in range(PACK)]
+        adv = [sbuf(f"adv{t}", [P, S], F32) for t in range(PACK)]
+        pgz = [sbuf(f"pgz{t}", [P, S], F32) for t in range(PACK)]
+        starts = [sum(CHUNKS[:c]) for c in range(len(CHUNKS))]
+        hid = [sbuf(f"hid{c}", [P, PACK, w], F32) for c, w in enumerate(CHUNKS)]
+
+        def control(t, c):
+            j0, w = starts[c], CHUNKS[c]
+            nc.vector.tensor_tensor(
+                hid[c][:, t, :],
+                adv[t][:].indirect(shuf_sb[:, j0 // 16 : (j0 + w) // 16]),
+                pgz[t][:, j0 : j0 + w],
+                ALU.add,
+            )
+
+        def by_group(ap):
+            return ap.rearrange("p (v d) -> p v d", d=D)
+
+        for t in range(PACK):
+            others = bank(2 * t, f"others{t}", [P, D, V])
+            own = bank(2 * t + 1, f"own{t}", [P, D, V])
+            for d in reversed(range(D)):
+                rest = [e for e in range(D) if e != d]
+                for e in rest:
+                    nc.tensor.matmul(
+                        others[:, d, :], lhsT=rew_t[e][:, t, :], rhs=ident[:], is_transpose=True,
+                        start=(e == rest[0]), stop=(e == rest[-1]),
+                    )
+            for d in range(D):
+                nc.tensor.transpose(own[:, d, :], rew_t[d][:, t, :], ident[:])
+            unit_t = unit_sb[:, t : t + 1]
+            nc.vector.scalar_tensor_tensor(
+                by_group(base[t][:]), others[:].rearrange("p d v -> p v d"), unit_t,
+                by_group(rden[t][:]), ALU.mult, ALU.mult,
+            )
+            nc.vector.scalar_tensor_tensor(
+                by_group(adv[t][:]), own[:].rearrange("p d v -> p v d"), unit_t,
+                by_group(base[t][:]), ALU.mult, ALU.subtract,
+            )
+
+        for t in range(PACK):
+            cols = slice(t * P, (t + 1) * P)
+            logp = bank(t, f"logp{t}", [P, S])
+            for o in range(PASSES):
+                nc.tensor.matmul_mx(
+                    out=logp[:],
+                    lhsT=w2q[o][:, cols].bitcast(FP8X4),
+                    lhsT_scale=w2s[o][:, cols],
+                    rhs=picked[o][:].bitcast(FP8X4),
+                    rhs_scale=picked_s[4 * o :, :],
+                    start=(o == 0),
+                    stop=(o == PASSES - 1),
+                )
+            nc.vector.tensor_tensor(pgz[t][:], logp[:], adv[t][:], ALU.mult)
+        for t in range(PACK):
+            control(t, 0)
+
+        w3g = sbuf("w3g", [P, N, PACK], BF16)
+        w3q = sbuf("w3q", [P, N], U32)
+        w3s = sbuf("w3s", [P, N], U8)
+        interleave(nc.scalar.copy, w3g, w3raw)
+        quantize(w3q[:], w3s[:], w3g[:].rearrange("p n j -> p (n j)"))
+
+        for c, w in enumerate(CHUNKS):
+            if c > 0:
+                for t in range(PACK):
+                    control(t, c)
+            hid_g = sbuf(f"hid_g{c}", [P, w, PACK], BF16)
+            interleave(nc.vector.tensor_copy if c == len(CHUNKS) - 1 else nc.scalar.copy, hid_g, hid[c])
+            hid_q = sbuf(f"hid_q{c}", [P, w], U32)
+            hid_s = sbuf(f"hid_s{c}", [P, w], U8)
+            quantize(hid_q[:], hid_s[:], hid_g[:].rearrange("p n j -> p (n j)"))
+            result = bank(D + c, f"result{c}", [P, w])
+            nc.tensor.matmul_mx(
+                out=result[:], lhsT=w3q[:].bitcast(FP8X4), lhsT_scale=w3s[:],
+                rhs=hid_q[:].bitcast(FP8X4), rhs_scale=hid_s[:], start=True, stop=True,
+            )
+            staged = sbuf(f"staged{c}", [P, w], F32)
+            nc.scalar.copy(staged[:], result[:])
+            nc.sync.dma_start(out=out[:, starts[c] : starts[c] + w], in_=staged[:])

@@ -21,6 +21,7 @@ PACK = 4
 PASSES = K // (P * PACK)
 V = S // D
 CHUNKS = (256, 128, 128)
+WARM_PASSES = 4
 
 
 def tile_picked_yrloov_pg_p_kernel(
@@ -78,20 +79,24 @@ def tile_picked_yrloov_pg_p_kernel(
 
         root = [sbuf(f"root{t}", [P, S], F32) for t in range(PACK)]
         rabs = [sbuf(f"rabs{t}", [P, S], F32) for t in range(PACK)]
-        sign = [sbuf(f"sign{t}", [P, S], F32) for t in range(PACK)]
-        rden = [sbuf(f"rden{t}", [P, S], F32) for t in range(PACK)]
+        half_sign = [sbuf(f"half_sign{h}", [P, 2, S], F32) for h in range(2)]
+        for h in range(2):
+            nc.vector.tensor_scalar(half_sign[h][:], den_sb[h][:], 0.0, 0.5, ALU.is_ge, ALU.subtract)
         for t in range(PACK):
-            den_t = den_sb[t // 2][:, t % 2, :]
-            nc.scalar.activation(root[t][:], den_t, ACT.Abs_reciprocal_sqrt)
+            nc.scalar.activation(root[t][:], den_sb[t // 2][:, t % 2, :], ACT.Abs_reciprocal_sqrt)
             nc.scalar.activation(rabs[t][:], root[t][:], ACT.Square)
-            nc.scalar.activation(sign[t][:], den_t, ACT.Sign)
-        warm = sbuf("warm", [P, 1], F32)
-        nc.scalar.activation(warm[:], root[PACK - 1][:, 0:1], ACT.Sigmoid)
 
-        def signed_reciprocal(t):
-            nc.vector.tensor_tensor(rden[t][:], rabs[t][:], sign[t][:], ALU.mult)
+        rden = {}
 
-        signed_reciprocal(0)
+        def signed_reciprocals(h, tag):
+            pair = keep.tile([P, 2, S], F32, name=f"rden{h}", tag=tag, align_bytes=64)
+            for i in range(2):
+                rden[2 * h + i] = pair[:, i, :]
+                nc.vector.scalar_tensor_tensor(
+                    pair[:, i, :], rabs[2 * h + i][:], 2.0, half_sign[h][:, i, :], ALU.mult, ALU.mult
+                )
+
+        signed_reciprocals(0, "rden0")
 
         picked = [sbuf(f"picked{o}", [P, S], U32) for o in range(PASSES)]
         dealt = [sbuf(f"dealt{o}", [P, D, V], U32) for o in range(PASSES)]
@@ -120,10 +125,11 @@ def tile_picked_yrloov_pg_p_kernel(
         def bank(b, name, shape):
             return psum.tile(shape, F32, name=name, tag=f"bank{b}")
 
-        w1q, w1s = {}, {}
+        w1g, w1q, w1s = {}, {}, {}
 
         def prepare_w1(h, o, engine_copy):
-            grouped = sbuf(f"w1g{h}{o}", [P, H // 2, PACK], BF16)
+            grouped = keep.tile([P, H // 2, PACK], BF16, name=f"w1g{h}{o}", tag=f"w1g{h}{o}", align_bytes=64)
+            w1g[h, o] = grouped
             interleave(engine_copy, grouped, w1raw[h, o])
             w1q[h, o] = sbuf(f"w1q{h}{o}", [P, H // 2], U32)
             w1s[h, o] = sbuf(f"w1s{h}{o}", [P, H // 2], U8)
@@ -131,43 +137,59 @@ def tile_picked_yrloov_pg_p_kernel(
 
         rew_t = [sbuf(f"rew_t{d}", [P, PACK, P], F32) for d in range(D)]
 
-        def rewards(h):
-            logits = [bank(D * h + d, f"logits{h}{d}", [P, H // 2]) for d in range(D)]
-            for o in range(PASSES):
-                for d in range(D):
-                    nc.tensor.matmul_mx(
-                        out=logits[d][:],
-                        lhsT=dealt[o][:, d, :].bitcast(FP8X4),
-                        lhsT_scale=dealt_s[4 * o :, d, :],
-                        rhs=w1q[h, o][:].bitcast(FP8X4),
-                        rhs_scale=w1s[h, o][:],
-                        start=(o == 0),
-                        stop=(o == PASSES - 1),
-                    )
-            for d in range(D):
-                nc.scalar.activation(
-                    rew_t[d][:, :, 64 * h : 64 * h + 64], logits[d][:].rearrange("p (m t) -> p t m", t=PACK), ACT.Sigmoid
-                )
+        def logit_pass(dst, h, d, o):
+            nc.tensor.matmul_mx(
+                out=dst,
+                lhsT=dealt[o][:, d, :].bitcast(FP8X4),
+                lhsT_scale=dealt_s[4 * o :, d, :],
+                rhs=w1q[h, o][:].bitcast(FP8X4),
+                rhs_scale=w1s[h, o][:],
+                start=(o == 0),
+                stop=(o == PASSES - 1),
+            )
+
+        def reward(src, h, d):
+            nc.scalar.activation(
+                rew_t[d][:, :, 64 * h : 64 * h + 64], src.rearrange("p (m t) -> p t m", t=PACK), ACT.Sigmoid
+            )
 
         pick_words(0)
         nc.vector.tensor_copy(picked_s[:], scale_table[:].indirect(offs_sb[:]))
         deal(dealt_s, picked_s)
-        prepare_w1(0, 0, nc.vector.tensor_copy)
+        prepare_w1(0, 0, nc.scalar.copy)
+        table_warm = sbuf("table_warm", [P, 1], F32)
+        nc.scalar.activation(table_warm[:], w1g[0, 0][:, 0, 0:1], ACT.Sigmoid)
+        clock_warm = bank(3, "clock_warm", [P, S])
+        for rep in range(WARM_PASSES):
+            nc.tensor.matmul_mx(
+                out=clock_warm[:], lhsT=w1q[0, 0][:, :P].bitcast(FP8X4), lhsT_scale=w1s[0, 0][:, :P],
+                rhs=picked[0][:].bitcast(FP8X4), rhs_scale=picked_s[:], start=True, stop=True,
+            )
         pick_words(1)
-        prepare_w1(0, 1, nc.vector.tensor_copy)
-        prepare_w1(1, 0, nc.scalar.copy)
-        rewards(0)
+        prepare_w1(0, 1, nc.scalar.copy)
+        prepare_w1(1, 0, nc.vector.tensor_copy)
+        first = [bank(b, f"logits0{b}", [P, 2, H // 2]) for b in range(2)]
+        for d in range(D):
+            for o in range(PASSES):
+                logit_pass(first[d // 2][:, d % 2, :], 0, d, o)
+        second = [bank(D + d, f"logits1{d}", [P, H // 2]) for d in range(D)]
+        for d in range(D):
+            logit_pass(second[d][:], 1, d, 0)
         prepare_w1(1, 1, nc.vector.tensor_copy)
-        rewards(1)
-        for t in range(1, PACK):
-            signed_reciprocal(t)
+        for d in range(D):
+            reward(first[d // 2][:, d % 2, :], 0, d)
+        for d in range(D):
+            logit_pass(second[d][:], 1, d, 1)
+        for d in range(D):
+            reward(second[d][:], 1, d)
+        signed_reciprocals(1, "w1g11")
 
         w2g = [sbuf(f"w2g{o}", [P, PACK, P, PACK], BF16) for o in range(PASSES)]
         w2q = [sbuf(f"w2q{o}", [P, H], U32) for o in range(PASSES)]
         w2s = [sbuf(f"w2s{o}", [P, H], U8) for o in range(PASSES)]
         for o in range(PASSES):
             for m0 in range(0, P, 32):
-                engine_copy = nc.vector.tensor_copy if (o == 0 and m0 < 64) else nc.scalar.copy
+                engine_copy = nc.vector.tensor_copy if o == 0 else nc.scalar.copy
                 cast_dealt(engine_copy, w2g[o], w2raw[o], m0, slice(m0, m0 + 32))
             quantize(w2q[o][:], w2s[o][:], w2g[o][:].rearrange("p t m j -> p (t m j)"))
 
@@ -189,31 +211,33 @@ def tile_picked_yrloov_pg_p_kernel(
         def by_group(ap):
             return ap.rearrange("p (v d) -> p v d", d=D)
 
+        own = [bank(t, f"own{t}", [P, D, V]) for t in range(PACK)]
+        others = [bank(D + t, f"others{t}", [P, D, V]) for t in range(PACK)]
+        for d in range(D - 1):
+            for t in range(PACK):
+                nc.tensor.transpose(own[t][:, d, :], rew_t[d][:, t, :], ident[:])
         for t in range(PACK):
-            others = bank(2 * t, f"others{t}", [P, D, V])
-            own = bank(2 * t + 1, f"own{t}", [P, D, V])
             for d in reversed(range(D)):
                 rest = [e for e in range(D) if e != d]
                 for e in rest:
                     nc.tensor.matmul(
-                        others[:, d, :], lhsT=rew_t[e][:, t, :], rhs=ident[:], is_transpose=True,
+                        others[t][:, d, :], lhsT=rew_t[e][:, t, :], rhs=ident[:], is_transpose=True,
                         start=(e == rest[0]), stop=(e == rest[-1]),
                     )
-            for d in range(D):
-                nc.tensor.transpose(own[:, d, :], rew_t[d][:, t, :], ident[:])
+            nc.tensor.transpose(own[t][:, D - 1, :], rew_t[D - 1][:, t, :], ident[:])
             unit_t = unit_sb[:, t : t + 1]
             nc.vector.scalar_tensor_tensor(
-                by_group(base[t][:]), others[:].rearrange("p d v -> p v d"), unit_t,
-                by_group(rden[t][:]), ALU.mult, ALU.mult,
+                by_group(base[t][:]), others[t][:].rearrange("p d v -> p v d"), unit_t,
+                by_group(rden[t]), ALU.mult, ALU.mult,
             )
             nc.vector.scalar_tensor_tensor(
-                by_group(adv[t][:]), own[:].rearrange("p d v -> p v d"), unit_t,
+                by_group(adv[t][:]), own[t][:].rearrange("p d v -> p v d"), unit_t,
                 by_group(base[t][:]), ALU.mult, ALU.subtract,
             )
 
         for t in range(PACK):
             cols = slice(t * P, (t + 1) * P)
-            logp = bank(t, f"logp{t}", [P, S])
+            logp = bank(D + t, f"logp{t}", [P, S])
             for o in range(PASSES):
                 nc.tensor.matmul_mx(
                     out=logp[:],
@@ -243,7 +267,7 @@ def tile_picked_yrloov_pg_p_kernel(
             hid_q = sbuf(f"hid_q{c}", [P, w], U32)
             hid_s = sbuf(f"hid_s{c}", [P, w], U8)
             quantize(hid_q[:], hid_s[:], hid_g[:].rearrange("p n j -> p (n j)"))
-            result = bank(D + c, f"result{c}", [P, w])
+            result = bank(c, f"result{c}", [P, w])
             nc.tensor.matmul_mx(
                 out=result[:], lhsT=w3q[:].bitcast(FP8X4), lhsT_scale=w3s[:],
                 rhs=hid_q[:].bitcast(FP8X4), rhs_scale=hid_s[:], start=True, stop=True,

@@ -4,7 +4,7 @@ import concourse.mybir as mybir
 from concourse.masks import make_identity
 
 K, T, S, D, N, H = 1024, 2048, 512, 4, 128, 512
-FLOPS = 2 * K * H * S * 2 + 2 * H * N * S
+FLOPS = 2 * (2 * K * H * S) + 2 * H * N * S
 
 F32 = mybir.dt.float32
 BF16 = mybir.dt.bfloat16
@@ -19,15 +19,22 @@ ALU = mybir.AluOpType
 P = 128
 PACK = 4
 PASSES = K // (P * PACK)
-V = S // D
-CHUNKS = (256, 128, 128)
-WARM_PASSES = 4
+PROMPTS = S // D
+QUADRANT = 32
+SCALE_ROWS = 4
+LIST_ROWS = 16
+NEAR = 4
+HALF = H // 2
+W2_PIECE = 32
+STRETCHES = (256, 128, 128)
 
 
 def tile_picked_yrloov_pg_p_kernel(
     tc, x_words, x_scales, w1, w2, den, unit, w3, offs, shuf, out
 ):
     nc = tc.nc
+    slots = range(PACK)
+    members = range(D)
     with ExitStack() as ctx:
         keep = ctx.enter_context(tc.tile_pool(name="keep", bufs=1))
         psum = ctx.enter_context(tc.psum_pool(name="psum", bufs=1))
@@ -35,19 +42,22 @@ def tile_picked_yrloov_pg_p_kernel(
         def sbuf(name, shape, dtype):
             return keep.tile(shape, dtype, name=name, align_bytes=64)
 
+        def bank(b, name, shape):
+            return psum.tile(shape, F32, name=name, tag=f"bank{b}")
+
         den_rows = den.rearrange("(p t) j -> p t j", t=PACK)
         den_sb = [sbuf(f"den{h}", [P, 2, S], F32) for h in range(2)]
         for h in range(2):
             nc.sync.dma_start(out=den_sb[h][:], in_=den_rows[:, 2 * h : 2 * h + 2, :])
-        offs_sb = keep.tile([P, S // 16], U16, name="offs_sb")
+        offs_sb = keep.tile([P, S // LIST_ROWS], U16, name="offs_sb")
         nc.sync.dma_start(offs_sb[:], offs)
 
         scale_table = sbuf("scale_table", [P, T], U8)
         nc.vector.memset(scale_table[:].bitcast(I32), 0)
-        for q in range(4):
+        for q in range(P // QUADRANT):
             nc.scalar.dma_start(
-                out=scale_table[32 * q : 32 * q + 4 * PASSES, :].bitcast(I32),
-                in_=x_scales[:, 4 * q : 4 * q + 4, :].bitcast(I32),
+                out=scale_table[QUADRANT * q : QUADRANT * q + SCALE_ROWS * PASSES, :].bitcast(I32),
+                in_=x_scales[:, SCALE_ROWS * q : SCALE_ROWS * (q + 1), :].bitcast(I32),
             )
         unit_sb = sbuf("unit_sb", [P, PACK], F32)
         nc.scalar.dma_start(out=unit_sb[:], in_=unit.rearrange("(p t) o -> p (t o)", t=PACK))
@@ -57,221 +67,207 @@ def tile_picked_yrloov_pg_p_kernel(
         word_table = [sbuf(f"word_table{o}", [P, T], I32) for o in range(PASSES)]
 
         def load_words(o):
-            nc.sync.dma_start(out=word_table[o][:], in_=x_words[o].rearrange("p n t -> p (n t)").bitcast(I32))
+            nc.sync.dma_start(out=word_table[o][:], in_=x_words[o].rearrange("p n j -> p (n j)").bitcast(I32))
 
-        def load_rows(name, w, o, cols):
-            raw = sbuf(name, [P, PACK, cols.stop - cols.start], F32)
+        def load_rows(name, w, o, c0, width):
+            raw = sbuf(name, [P, PACK, width], F32)
             rows = w[o * P * PACK : (o + 1) * P * PACK, :].rearrange("(p j) c -> p j c", j=PACK)
-            nc.sync.dma_start(out=raw[:], in_=rows[:, :, cols])
+            nc.sync.dma_start(out=raw[:], in_=rows[:, :, c0 : c0 + width])
             return raw
 
-        halves = [slice(h * H // 2, (h + 1) * H // 2) for h in range(2)]
-        w1raw = {}
-        load_words(0)
-        w1raw[0, 0] = load_rows("w1raw00", w1, 0, halves[0])
-        load_words(1)
-        for h, o in ((0, 1), (1, 0), (1, 1)):
-            w1raw[h, o] = load_rows(f"w1raw{h}{o}", w1, o, halves[h])
-        w2raw = [load_rows(f"w2raw{o}", w2, o, slice(0, H)) for o in range(PASSES)]
-        w3raw = load_rows("w3raw", w3, 0, slice(0, N))
-        shuf_sb = keep.tile([P, S // 16], U16, name="shuf_sb")
+        w1_raw = {}
+        for h in range(2):
+            for o in range(PASSES):
+                if h == 0:
+                    load_words(o)
+                w1_raw[h, o] = load_rows(f"w1_raw{h}{o}", w1, o, h * HALF, HALF)
+        w2_raw = [load_rows(f"w2_raw{o}", w2, o, 0, H) for o in range(PASSES)]
+        w3_raw = load_rows("w3_raw", w3, 0, 0, N)
+        shuf_sb = keep.tile([P, S // LIST_ROWS], U16, name="shuf_sb")
         nc.sync.dma_start(shuf_sb[:], shuf)
 
-        root = [sbuf(f"root{t}", [P, S], F32) for t in range(PACK)]
-        rabs = [sbuf(f"rabs{t}", [P, S], F32) for t in range(PACK)]
+        root = [sbuf(f"root{t}", [P, S], F32) for t in slots]
+        rabs = [sbuf(f"rabs{t}", [P, S], F32) for t in slots]
+        rden = [sbuf(f"rden{t}", [P, S], F32) for t in slots]
         half_sign = [sbuf(f"half_sign{h}", [P, 2, S], F32) for h in range(2)]
         for h in range(2):
             nc.vector.tensor_scalar(half_sign[h][:], den_sb[h][:], 0.0, 0.5, ALU.is_ge, ALU.subtract)
-        for t in range(PACK):
+        for t in slots:
             nc.scalar.activation(root[t][:], den_sb[t // 2][:, t % 2, :], ACT.Abs_reciprocal_sqrt)
             nc.scalar.activation(rabs[t][:], root[t][:], ACT.Square)
-
-        rden = {}
-
-        def signed_reciprocals(h, tag):
-            pair = keep.tile([P, 2, S], F32, name=f"rden{h}", tag=tag, align_bytes=64)
-            for i in range(2):
-                rden[2 * h + i] = pair[:, i, :]
-                nc.vector.scalar_tensor_tensor(
-                    pair[:, i, :], rabs[2 * h + i][:], 2.0, half_sign[h][:, i, :], ALU.mult, ALU.mult
-                )
-
-        signed_reciprocals(0, "rden0")
-
-        picked = [sbuf(f"picked{o}", [P, S], U32) for o in range(PASSES)]
-        dealt = [sbuf(f"dealt{o}", [P, D, V], U32) for o in range(PASSES)]
-        picked_s = sbuf("picked_s", [P, S], U8)
-        dealt_s = sbuf("dealt_s", [P, D, V], U8)
-
-        def deal(dst, src):
-            nc.vector.tensor_copy(dst[:].rearrange("p d v -> p v d"), src[:].rearrange("p (v d) -> p v d", d=D))
-
-        def pick_words(o):
-            nc.vector.tensor_copy(picked[o][:], word_table[o][:].bitcast(U32).indirect(offs_sb[:]))
-            deal(dealt[o], picked[o])
-
-        def cast_dealt(engine_copy, grouped, raw, m0, src_m):
-            width = src_m.stop - src_m.start
-            dst = grouped[:].rearrange("p t m j -> p m j t")[:, m0 : m0 + width]
-            src = raw[:].rearrange("p j (m t) -> p m j t", t=PACK)[:, src_m]
-            engine_copy(dst, src)
-
-        def quantize(words, scales, values):
-            nc.vector.quantize_mx(out=words.bitcast(FP8X4), scales=scales, in_=values)
-
-        def interleave(engine_copy, dst, src):
-            engine_copy(dst[:].rearrange("p (c i) t -> p c t i", i=4), src[:].rearrange("p t (c i) -> p c t i", i=4))
-
-        def bank(b, name, shape):
-            return psum.tile(shape, F32, name=name, tag=f"bank{b}")
-
-        w1g, w1q, w1s = {}, {}, {}
-
-        def prepare_w1(h, o, engine_copy):
-            grouped = keep.tile([P, H // 2, PACK], BF16, name=f"w1g{h}{o}", tag=f"w1g{h}{o}", align_bytes=64)
-            w1g[h, o] = grouped
-            interleave(engine_copy, grouped, w1raw[h, o])
-            w1q[h, o] = sbuf(f"w1q{h}{o}", [P, H // 2], U32)
-            w1s[h, o] = sbuf(f"w1s{h}{o}", [P, H // 2], U8)
-            quantize(w1q[h, o][:], w1s[h, o][:], grouped[:].rearrange("p n j -> p (n j)"))
-
-        rew_t = [sbuf(f"rew_t{d}", [P, PACK, P], F32) for d in range(D)]
-
-        def logit_pass(dst, h, d, o):
-            nc.tensor.matmul_mx(
-                out=dst,
-                lhsT=dealt[o][:, d, :].bitcast(FP8X4),
-                lhsT_scale=dealt_s[4 * o :, d, :],
-                rhs=w1q[h, o][:].bitcast(FP8X4),
-                rhs_scale=w1s[h, o][:],
-                start=(o == 0),
-                stop=(o == PASSES - 1),
+            nc.vector.scalar_tensor_tensor(
+                rden[t][:], rabs[t][:], 2.0, half_sign[t // 2][:, t % 2, :], ALU.mult, ALU.mult
             )
 
-        def reward(src, h, d):
-            nc.scalar.activation(
-                rew_t[d][:, :, 64 * h : 64 * h + 64], src.rearrange("p (m t) -> p t m", t=PACK), ACT.Sigmoid
-            )
+        picked_words = [sbuf(f"picked_words{o}", [P, S], U32) for o in range(PASSES)]
+        dealt_words = [sbuf(f"dealt_words{o}", [P, D, PROMPTS], U32) for o in range(PASSES)]
+        picked_scales = sbuf("picked_scales", [P, S], U8)
+        dealt_scales = sbuf("dealt_scales", [P, D, PROMPTS], U8)
 
-        pick_words(0)
-        nc.vector.tensor_copy(picked_s[:], scale_table[:].indirect(offs_sb[:]))
-        deal(dealt_s, picked_s)
-        prepare_w1(0, 0, nc.scalar.copy)
-        table_warm = sbuf("table_warm", [P, 1], F32)
-        nc.scalar.activation(table_warm[:], w1g[0, 0][:, 0, 0:1], ACT.Sigmoid)
-        clock_warm = bank(3, "clock_warm", [P, S])
-        for rep in range(WARM_PASSES):
-            nc.tensor.matmul_mx(
-                out=clock_warm[:], lhsT=w1q[0, 0][:, :P].bitcast(FP8X4), lhsT_scale=w1s[0, 0][:, :P],
-                rhs=picked[0][:].bitcast(FP8X4), rhs_scale=picked_s[:], start=True, stop=True,
-            )
-        pick_words(1)
-        prepare_w1(0, 1, nc.scalar.copy)
-        prepare_w1(1, 0, nc.vector.tensor_copy)
-        first = [bank(b, f"logits0{b}", [P, 2, H // 2]) for b in range(2)]
-        for d in range(D):
-            for o in range(PASSES):
-                logit_pass(first[d // 2][:, d % 2, :], 0, d, o)
-        second = [bank(D + d, f"logits1{d}", [P, H // 2]) for d in range(D)]
-        for d in range(D):
-            logit_pass(second[d][:], 1, d, 0)
-        prepare_w1(1, 1, nc.vector.tensor_copy)
-        for d in range(D):
-            reward(first[d // 2][:, d % 2, :], 0, d)
-        for d in range(D):
-            logit_pass(second[d][:], 1, d, 1)
-        for d in range(D):
-            reward(second[d][:], 1, d)
-        signed_reciprocals(1, "w1g11")
-
-        w2g = [sbuf(f"w2g{o}", [P, PACK, P, PACK], BF16) for o in range(PASSES)]
-        w2q = [sbuf(f"w2q{o}", [P, H], U32) for o in range(PASSES)]
-        w2s = [sbuf(f"w2s{o}", [P, H], U8) for o in range(PASSES)]
-        for o in range(PASSES):
-            for m0 in range(0, P, 32):
-                engine_copy = nc.vector.tensor_copy if o == 0 else nc.scalar.copy
-                cast_dealt(engine_copy, w2g[o], w2raw[o], m0, slice(m0, m0 + 32))
-            quantize(w2q[o][:], w2s[o][:], w2g[o][:].rearrange("p t m j -> p (t m j)"))
-
-        base = [sbuf(f"base{t}", [P, S], F32) for t in range(PACK)]
-        adv = [sbuf(f"adv{t}", [P, S], F32) for t in range(PACK)]
-        pgz = [sbuf(f"pgz{t}", [P, S], F32) for t in range(PACK)]
-        starts = [sum(CHUNKS[:c]) for c in range(len(CHUNKS))]
-        hid = [sbuf(f"hid{c}", [P, PACK, w], F32) for c, w in enumerate(CHUNKS)]
-
-        def control(t, c):
-            j0, w = starts[c], CHUNKS[c]
-            nc.vector.tensor_tensor(
-                hid[c][:, t, :],
-                adv[t][:].indirect(shuf_sb[:, j0 // 16 : (j0 + w) // 16]),
-                pgz[t][:, j0 : j0 + w],
-                ALU.add,
-            )
-
-        def by_group(ap):
+        def by_prompt(ap):
             return ap.rearrange("p (v d) -> p v d", d=D)
 
-        own = [bank(t, f"own{t}", [P, D, V]) for t in range(PACK)]
-        others = [bank(D + t, f"others{t}", [P, D, V]) for t in range(PACK)]
-        for d in range(D - 1):
-            for t in range(PACK):
-                nc.tensor.transpose(own[t][:, d, :], rew_t[d][:, t, :], ident[:])
-        for t in range(PACK):
-            for d in reversed(range(D)):
-                rest = [e for e in range(D) if e != d]
-                for e in rest:
-                    nc.tensor.matmul(
-                        others[t][:, d, :], lhsT=rew_t[e][:, t, :], rhs=ident[:], is_transpose=True,
-                        start=(e == rest[0]), stop=(e == rest[-1]),
-                    )
-            nc.tensor.transpose(own[t][:, D - 1, :], rew_t[D - 1][:, t, :], ident[:])
-            unit_t = unit_sb[:, t : t + 1]
-            nc.vector.scalar_tensor_tensor(
-                by_group(base[t][:]), others[t][:].rearrange("p d v -> p v d"), unit_t,
-                by_group(rden[t]), ALU.mult, ALU.mult,
-            )
-            nc.vector.scalar_tensor_tensor(
-                by_group(adv[t][:]), own[t][:].rearrange("p d v -> p v d"), unit_t,
-                by_group(base[t][:]), ALU.mult, ALU.subtract,
+        def member_last(ap):
+            return ap.rearrange("p d v -> p v d")
+
+        def pick_words(o):
+            nc.vector.tensor_copy(picked_words[o][:], word_table[o][:].bitcast(U32).indirect(offs_sb[:]))
+            nc.vector.tensor_copy(member_last(dealt_words[o][:]), by_prompt(picked_words[o][:]))
+
+        def quantize(words, scales, values):
+            nc.vector.quantize_mx(out=words[:].bitcast(FP8X4), scales=scales[:], in_=values)
+
+        def interleave(copy, grouped, rows):
+            copy(
+                grouped[:].rearrange("p (c n) j -> p c j n", n=NEAR),
+                rows[:].rearrange("p j (c n) -> p c j n", n=NEAR),
             )
 
-        for t in range(PACK):
-            cols = slice(t * P, (t + 1) * P)
-            logp = bank(D + t, f"logp{t}", [P, S])
-            for o in range(PASSES):
+        w1_grouped, w1_words, w1_scales = {}, {}, {}
+
+        def prepare_w1(h, o, copy):
+            w1_grouped[h, o] = sbuf(f"w1_grouped{h}{o}", [P, HALF, PACK], BF16)
+            interleave(copy, w1_grouped[h, o], w1_raw[h, o])
+            w1_words[h, o] = sbuf(f"w1_words{h}{o}", [P, HALF], U32)
+            w1_scales[h, o] = sbuf(f"w1_scales{h}{o}", [P, HALF], U8)
+            quantize(w1_words[h, o], w1_scales[h, o], w1_grouped[h, o][:].rearrange("p c j -> p (c j)"))
+
+        rew_t = [sbuf(f"rew_t{d}", [P, PACK, P], F32) for d in members]
+        logits = {(h, d): bank(D * h + d, f"logits{h}{d}", [P, HALF]) for h in range(2) for d in members}
+
+        def logit_passes(h, o):
+            for d in members:
                 nc.tensor.matmul_mx(
-                    out=logp[:],
-                    lhsT=w2q[o][:, cols].bitcast(FP8X4),
-                    lhsT_scale=w2s[o][:, cols],
-                    rhs=picked[o][:].bitcast(FP8X4),
-                    rhs_scale=picked_s[4 * o :, :],
+                    out=logits[h, d][:],
+                    lhsT=dealt_words[o][:, d, :].bitcast(FP8X4),
+                    lhsT_scale=dealt_scales[SCALE_ROWS * o :, d, :],
+                    rhs=w1_words[h, o][:].bitcast(FP8X4),
+                    rhs_scale=w1_scales[h, o][:],
                     start=(o == 0),
                     stop=(o == PASSES - 1),
                 )
-            nc.vector.tensor_tensor(pgz[t][:], logp[:], adv[t][:], ALU.mult)
-        for t in range(PACK):
-            control(t, 0)
 
-        w3g = sbuf("w3g", [P, N, PACK], BF16)
-        w3q = sbuf("w3q", [P, N], U32)
-        w3s = sbuf("w3s", [P, N], U8)
-        interleave(nc.scalar.copy, w3g, w3raw)
-        quantize(w3q[:], w3s[:], w3g[:].rearrange("p n j -> p (n j)"))
+        def rewards(h, some_slots):
+            for d in members:
+                nc.scalar.activation(
+                    rew_t[d][:, some_slots, h * P // 2 : (h + 1) * P // 2],
+                    logits[h, d][:].rearrange("v (p t) -> v t p", t=PACK)[:, some_slots],
+                    ACT.Sigmoid,
+                )
 
-        for c, w in enumerate(CHUNKS):
-            if c > 0:
-                for t in range(PACK):
-                    control(t, c)
-            hid_g = sbuf(f"hid_g{c}", [P, w, PACK], BF16)
-            interleave(nc.vector.tensor_copy if c == len(CHUNKS) - 1 else nc.scalar.copy, hid_g, hid[c])
-            hid_q = sbuf(f"hid_q{c}", [P, w], U32)
-            hid_s = sbuf(f"hid_s{c}", [P, w], U8)
-            quantize(hid_q[:], hid_s[:], hid_g[:].rearrange("p n j -> p (n j)"))
-            result = bank(c, f"result{c}", [P, w])
-            nc.tensor.matmul_mx(
-                out=result[:], lhsT=w3q[:].bitcast(FP8X4), lhsT_scale=w3s[:],
-                rhs=hid_q[:].bitcast(FP8X4), rhs_scale=hid_s[:], start=True, stop=True,
+        nc.vector.tensor_copy(picked_scales[:], scale_table[:].indirect(offs_sb[:]))
+        nc.vector.tensor_copy(dealt_scales[:], picked_scales[:].rearrange("p (v d) -> p d v", d=D))
+        pick_words(0)
+        prepare_w1(0, 0, nc.scalar.copy)
+        table_load = sbuf("table_load", [P, 1], F32)
+        nc.scalar.activation(table_load[:], w1_grouped[0, 0][:, 0, 0:1], ACT.Sigmoid)
+        logit_passes(0, 0)
+        pick_words(1)
+        prepare_w1(0, 1, nc.scalar.copy)
+        logit_passes(0, 1)
+        prepare_w1(1, 0, nc.scalar.copy)
+        logit_passes(1, 0)
+        rewards(0, slice(0, PACK))
+        prepare_w1(1, 1, nc.vector.tensor_copy)
+        logit_passes(1, 1)
+        rewards(1, slice(0, 1))
+        rewards(1, slice(1, PACK))
+
+        w2_grouped = [sbuf(f"w2_grouped{o}", [P, PACK, P, PACK], BF16) for o in range(PASSES)]
+        w2_words = [sbuf(f"w2_words{o}", [P, H], U32) for o in range(PASSES)]
+        w2_scales = [sbuf(f"w2_scales{o}", [P, H], U8) for o in range(PASSES)]
+        for o, copy in enumerate((nc.vector.tensor_copy, nc.scalar.copy)):
+            for m0 in range(0, P, W2_PIECE):
+                copy(
+                    w2_grouped[o][:].rearrange("p t m j -> p m j t")[:, m0 : m0 + W2_PIECE],
+                    w2_raw[o][:].rearrange("p j (m t) -> p m j t", t=PACK)[:, m0 : m0 + W2_PIECE],
+                )
+            quantize(w2_words[o], w2_scales[o], w2_grouped[o][:].rearrange("p t m j -> p (t m j)"))
+
+        base = [sbuf(f"base{t}", [P, S], F32) for t in slots]
+        adv = [sbuf(f"adv{t}", [P, S], F32) for t in slots]
+        pgz = [sbuf(f"pgz{t}", [P, S], F32) for t in slots]
+        starts = [sum(STRETCHES[:c]) for c in range(len(STRETCHES))]
+        hid = [sbuf(f"hid{c}", [P, PACK, width], F32) for c, width in enumerate(STRETCHES)]
+        others = [bank(2 * t, f"others{t}", [P, D, PROMPTS]) for t in slots]
+        own = [bank(2 * t + 1, f"own{t}", [P, D, PROMPTS]) for t in slots]
+
+        def add_control(t, c):
+            j0, j1 = starts[c], starts[c] + STRETCHES[c]
+            places = shuf_sb[:, j0 // LIST_ROWS : j1 // LIST_ROWS]
+            nc.vector.tensor_tensor(hid[c][:, t, :], adv[t][:].indirect(places), pgz[t][:, j0:j1], ALU.add)
+
+        def advantage(t):
+            for d in reversed(members):
+                rest = [e for e in members if e != d]
+                for e in rest:
+                    nc.tensor.matmul(
+                        others[t][:, d, :],
+                        lhsT=rew_t[e][:, t, :],
+                        rhs=ident[:],
+                        is_transpose=True,
+                        start=(e == rest[0]),
+                        stop=(e == rest[-1]),
+                    )
+            for d in members:
+                nc.tensor.transpose(own[t][:, d, :], rew_t[d][:, t, :], ident[:])
+            unit_t = unit_sb[:, t : t + 1]
+            nc.vector.scalar_tensor_tensor(
+                by_prompt(base[t][:]), member_last(others[t][:]), unit_t, by_prompt(rden[t][:]), ALU.mult, ALU.mult
             )
-            staged = sbuf(f"staged{c}", [P, w], F32)
+            nc.vector.scalar_tensor_tensor(
+                by_prompt(adv[t][:]), member_last(own[t][:]), unit_t, by_prompt(base[t][:]), ALU.mult, ALU.subtract
+            )
+
+        def gradient(t):
+            cols = slice(t * P, (t + 1) * P)
+            yl = bank(t, f"yl{t}", [P, S])
+            for o in range(PASSES):
+                nc.tensor.matmul_mx(
+                    out=yl[:],
+                    lhsT=w2_words[o][:, cols].bitcast(FP8X4),
+                    lhsT_scale=w2_scales[o][:, cols],
+                    rhs=picked_words[o][:].bitcast(FP8X4),
+                    rhs_scale=picked_scales[SCALE_ROWS * o :, :],
+                    start=(o == 0),
+                    stop=(o == PASSES - 1),
+                )
+            nc.vector.tensor_tensor(pgz[t][:], yl[:], adv[t][:], ALU.mult)
+
+        def first_stretch(t):
+            add_control(t, 0)
+
+        for t0 in range(0, PACK, 2):
+            for stage in (advantage, gradient, first_stretch):
+                for t in (t0, t0 + 1):
+                    stage(t)
+
+        w3_grouped = sbuf("w3_grouped", [P, N, PACK], BF16)
+        w3_words = sbuf("w3_words", [P, N], U32)
+        w3_scales = sbuf("w3_scales", [P, N], U8)
+        interleave(nc.scalar.copy, w3_grouped, w3_raw)
+        quantize(w3_words, w3_scales, w3_grouped[:].rearrange("p c j -> p (c j)"))
+
+        for c, width in enumerate(STRETCHES):
+            if c > 0:
+                for t in slots:
+                    add_control(t, c)
+            hid_grouped = sbuf(f"hid_grouped{c}", [P, width, PACK], BF16)
+            is_last = c == len(STRETCHES) - 1
+            interleave(nc.vector.tensor_copy if is_last else nc.scalar.copy, hid_grouped, hid[c])
+            hid_words = sbuf(f"hid_words{c}", [P, width], U32)
+            hid_scales = sbuf(f"hid_scales{c}", [P, width], U8)
+            quantize(hid_words, hid_scales, hid_grouped[:].rearrange("p c j -> p (c j)"))
+            result = bank(PACK + c, f"result{c}", [P, width])
+            nc.tensor.matmul_mx(
+                out=result[:],
+                lhsT=w3_words[:].bitcast(FP8X4),
+                lhsT_scale=w3_scales[:],
+                rhs=hid_words[:].bitcast(FP8X4),
+                rhs_scale=hid_scales[:],
+                start=True,
+                stop=True,
+            )
+            staged = sbuf(f"staged{c}", [P, width], F32)
             nc.scalar.copy(staged[:], result[:])
-            nc.sync.dma_start(out=out[:, starts[c] : starts[c] + w], in_=staged[:])
+            nc.sync.dma_start(out=out[:, starts[c] : starts[c] + width], in_=staged[:])

from contextlib import ExitStack

import concourse.mybir as mybir
from concourse.masks import make_identity

K, T, S, D, N, H = 1024, 2048, 512, 4, 128, 512
FLOPS = 2 * (2 * K * H * S) + 2 * H * N * S

F32 = mybir.dt.float32
BF16 = mybir.dt.bfloat16
I32 = mybir.dt.int32
U32 = mybir.dt.uint32
U16 = mybir.dt.uint16
U8 = mybir.dt.uint8
FP8X4 = mybir.dt.float8_e4m3fn_x4
ACT = mybir.ActivationFunctionType
ALU = mybir.AluOpType

P = 128
PACK = 4
PASSES = K // (P * PACK)
PROMPTS = S // D
QUADRANT = 32
SCALE_ROWS = 4
LIST_ROWS = 16
NEAR = 4
HALF = H // 2
W2_PIECE = 32
STRETCHES = (256, 128, 128)


def tile_picked_yrloov_pg_p_kernel(
    tc, x_words, x_scales, w1, w2, den, unit, w3, offs, shuf, out
):
    nc = tc.nc
    slots = range(PACK)
    members = range(D)
    with ExitStack() as ctx:
        keep = ctx.enter_context(tc.tile_pool(name="keep", bufs=1))
        psum = ctx.enter_context(tc.psum_pool(name="psum", bufs=1))

        def sbuf(name, shape, dtype):
            return keep.tile(shape, dtype, name=name, align_bytes=64)

        def bank(b, name, shape):
            return psum.tile(shape, F32, name=name, tag=f"bank{b}")

        den_rows = den.rearrange("(p t) j -> p t j", t=PACK)
        den_sb = [sbuf(f"den{h}", [P, 2, S], F32) for h in range(2)]
        for h in range(2):
            nc.sync.dma_start(out=den_sb[h][:], in_=den_rows[:, 2 * h : 2 * h + 2, :])
        offs_sb = keep.tile([P, S // LIST_ROWS], U16, name="offs_sb")
        nc.sync.dma_start(offs_sb[:], offs)

        scale_table = sbuf("scale_table", [P, T], U8)
        nc.vector.memset(scale_table[:].bitcast(I32), 0)
        for q in range(P // QUADRANT):
            nc.scalar.dma_start(
                out=scale_table[QUADRANT * q : QUADRANT * q + SCALE_ROWS * PASSES, :].bitcast(I32),
                in_=x_scales[:, SCALE_ROWS * q : SCALE_ROWS * (q + 1), :].bitcast(I32),
            )
        unit_sb = sbuf("unit_sb", [P, PACK], F32)
        nc.scalar.dma_start(out=unit_sb[:], in_=unit.rearrange("(p t) o -> p (t o)", t=PACK))
        ident = sbuf("ident", [P, P], F32)
        make_identity(nc, ident[:])

        word_table = [sbuf(f"word_table{o}", [P, T], I32) for o in range(PASSES)]

        def load_words(o):
            nc.sync.dma_start(out=word_table[o][:], in_=x_words[o].rearrange("p n j -> p (n j)").bitcast(I32))

        def load_rows(name, w, o, c0, width):
            raw = sbuf(name, [P, PACK, width], F32)
            rows = w[o * P * PACK : (o + 1) * P * PACK, :].rearrange("(p j) c -> p j c", j=PACK)
            nc.sync.dma_start(out=raw[:], in_=rows[:, :, c0 : c0 + width])
            return raw

        w1_raw = {}
        for h in range(2):
            for o in range(PASSES):
                if h == 0:
                    load_words(o)
                w1_raw[h, o] = load_rows(f"w1_raw{h}{o}", w1, o, h * HALF, HALF)
        w2_raw = [load_rows(f"w2_raw{o}", w2, o, 0, H) for o in range(PASSES)]
        w3_raw = load_rows("w3_raw", w3, 0, 0, N)
        shuf_sb = keep.tile([P, S // LIST_ROWS], U16, name="shuf_sb")
        nc.sync.dma_start(shuf_sb[:], shuf)

        root = [sbuf(f"root{t}", [P, S], F32) for t in slots]
        rabs = [sbuf(f"rabs{t}", [P, S], F32) for t in slots]
        rden = [sbuf(f"rden{t}", [P, S], F32) for t in slots]
        half_sign = [sbuf(f"half_sign{h}", [P, 2, S], F32) for h in range(2)]
        for h in range(2):
            nc.vector.tensor_scalar(half_sign[h][:], den_sb[h][:], 0.0, 0.5, ALU.is_ge, ALU.subtract)
        for t in slots:
            nc.scalar.activation(root[t][:], den_sb[t // 2][:, t % 2, :], ACT.Abs_reciprocal_sqrt)
            nc.scalar.activation(rabs[t][:], root[t][:], ACT.Square)
            nc.vector.scalar_tensor_tensor(
                rden[t][:], rabs[t][:], 2.0, half_sign[t // 2][:, t % 2, :], ALU.mult, ALU.mult
            )

        picked_words = [sbuf(f"picked_words{o}", [P, S], U32) for o in range(PASSES)]
        dealt_words = [sbuf(f"dealt_words{o}", [P, D, PROMPTS], U32) for o in range(PASSES)]
        picked_scales = sbuf("picked_scales", [P, S], U8)
        dealt_scales = sbuf("dealt_scales", [P, D, PROMPTS], U8)

        def by_prompt(ap):
            return ap.rearrange("p (v d) -> p v d", d=D)

        def member_last(ap):
            return ap.rearrange("p d v -> p v d")

        def pick_words(o):
            nc.vector.tensor_copy(picked_words[o][:], word_table[o][:].bitcast(U32).indirect(offs_sb[:]))
            nc.vector.tensor_copy(member_last(dealt_words[o][:]), by_prompt(picked_words[o][:]))

        def quantize(words, scales, values):
            nc.vector.quantize_mx(out=words[:].bitcast(FP8X4), scales=scales[:], in_=values)

        def interleave(copy, grouped, rows):
            copy(
                grouped[:].rearrange("p (c n) j -> p c j n", n=NEAR),
                rows[:].rearrange("p j (c n) -> p c j n", n=NEAR),
            )

        w1_grouped, w1_words, w1_scales = {}, {}, {}

        def prepare_w1(h, o, copy):
            w1_grouped[h, o] = sbuf(f"w1_grouped{h}{o}", [P, HALF, PACK], BF16)
            interleave(copy, w1_grouped[h, o], w1_raw[h, o])
            w1_words[h, o] = sbuf(f"w1_words{h}{o}", [P, HALF], U32)
            w1_scales[h, o] = sbuf(f"w1_scales{h}{o}", [P, HALF], U8)
            quantize(w1_words[h, o], w1_scales[h, o], w1_grouped[h, o][:].rearrange("p c j -> p (c j)"))

        rew_t = [sbuf(f"rew_t{d}", [P, PACK, P], F32) for d in members]
        logits = {(h, d): bank(D * h + d, f"logits{h}{d}", [P, HALF]) for h in range(2) for d in members}

        def logit_passes(h, o):
            for d in members:
                nc.tensor.matmul_mx(
                    out=logits[h, d][:],
                    lhsT=dealt_words[o][:, d, :].bitcast(FP8X4),
                    lhsT_scale=dealt_scales[SCALE_ROWS * o :, d, :],
                    rhs=w1_words[h, o][:].bitcast(FP8X4),
                    rhs_scale=w1_scales[h, o][:],
                    start=(o == 0),
                    stop=(o == PASSES - 1),
                )

        def rewards(h, some_slots):
            for d in members:
                nc.scalar.activation(
                    rew_t[d][:, some_slots, h * P // 2 : (h + 1) * P // 2],
                    logits[h, d][:].rearrange("v (p t) -> v t p", t=PACK)[:, some_slots],
                    ACT.Sigmoid,
                )

        nc.vector.tensor_copy(picked_scales[:], scale_table[:].indirect(offs_sb[:]))
        nc.vector.tensor_copy(dealt_scales[:], picked_scales[:].rearrange("p (v d) -> p d v", d=D))
        pick_words(0)
        prepare_w1(0, 0, nc.scalar.copy)
        table_load = sbuf("table_load", [P, 1], F32)
        nc.scalar.activation(table_load[:], w1_grouped[0, 0][:, 0, 0:1], ACT.Sigmoid)
        logit_passes(0, 0)
        pick_words(1)
        prepare_w1(0, 1, nc.scalar.copy)
        logit_passes(0, 1)
        prepare_w1(1, 0, nc.scalar.copy)
        logit_passes(1, 0)
        rewards(0, slice(0, PACK))
        prepare_w1(1, 1, nc.vector.tensor_copy)
        logit_passes(1, 1)
        rewards(1, slice(0, 1))
        rewards(1, slice(1, PACK))

        w2_grouped = [sbuf(f"w2_grouped{o}", [P, PACK, P, PACK], BF16) for o in range(PASSES)]
        w2_words = [sbuf(f"w2_words{o}", [P, H], U32) for o in range(PASSES)]
        w2_scales = [sbuf(f"w2_scales{o}", [P, H], U8) for o in range(PASSES)]
        for o, copy in enumerate((nc.vector.tensor_copy, nc.scalar.copy)):
            for m0 in range(0, P, W2_PIECE):
                copy(
                    w2_grouped[o][:].rearrange("p t m j -> p m j t")[:, m0 : m0 + W2_PIECE],
                    w2_raw[o][:].rearrange("p j (m t) -> p m j t", t=PACK)[:, m0 : m0 + W2_PIECE],
                )
            quantize(w2_words[o], w2_scales[o], w2_grouped[o][:].rearrange("p t m j -> p (t m j)"))

        base = [sbuf(f"base{t}", [P, S], F32) for t in slots]
        adv = [sbuf(f"adv{t}", [P, S], F32) for t in slots]
        pgz = [sbuf(f"pgz{t}", [P, S], F32) for t in slots]
        starts = [sum(STRETCHES[:c]) for c in range(len(STRETCHES))]
        hid = [sbuf(f"hid{c}", [P, PACK, width], F32) for c, width in enumerate(STRETCHES)]
        others = [bank(2 * t, f"others{t}", [P, D, PROMPTS]) for t in slots]
        own = [bank(2 * t + 1, f"own{t}", [P, D, PROMPTS]) for t in slots]

        def add_control(t, c):
            j0, j1 = starts[c], starts[c] + STRETCHES[c]
            places = shuf_sb[:, j0 // LIST_ROWS : j1 // LIST_ROWS]
            nc.vector.tensor_tensor(hid[c][:, t, :], adv[t][:].indirect(places), pgz[t][:, j0:j1], ALU.add)

        def advantage(t):
            for d in reversed(members):
                rest = [e for e in members if e != d]
                for e in rest:
                    nc.tensor.matmul(
                        others[t][:, d, :],
                        lhsT=rew_t[e][:, t, :],
                        rhs=ident[:],
                        is_transpose=True,
                        start=(e == rest[0]),
                        stop=(e == rest[-1]),
                    )
            for d in members:
                nc.tensor.transpose(own[t][:, d, :], rew_t[d][:, t, :], ident[:])
            unit_t = unit_sb[:, t : t + 1]
            nc.vector.scalar_tensor_tensor(
                by_prompt(base[t][:]), member_last(others[t][:]), unit_t, by_prompt(rden[t][:]), ALU.mult, ALU.mult
            )
            nc.vector.scalar_tensor_tensor(
                by_prompt(adv[t][:]), member_last(own[t][:]), unit_t, by_prompt(base[t][:]), ALU.mult, ALU.subtract
            )

        def gradient(t):
            cols = slice(t * P, (t + 1) * P)
            yl = bank(t, f"yl{t}", [P, S])
            for o in range(PASSES):
                nc.tensor.matmul_mx(
                    out=yl[:],
                    lhsT=w2_words[o][:, cols].bitcast(FP8X4),
                    lhsT_scale=w2_scales[o][:, cols],
                    rhs=picked_words[o][:].bitcast(FP8X4),
                    rhs_scale=picked_scales[SCALE_ROWS * o :, :],
                    start=(o == 0),
                    stop=(o == PASSES - 1),
                )
            nc.vector.tensor_tensor(pgz[t][:], yl[:], adv[t][:], ALU.mult)

        def first_stretch(t):
            add_control(t, 0)

        for t0 in range(0, PACK, 2):
            for stage in (advantage, gradient, first_stretch):
                for t in (t0, t0 + 1):
                    stage(t)

        w3_grouped = sbuf("w3_grouped", [P, N, PACK], BF16)
        w3_words = sbuf("w3_words", [P, N], U32)
        w3_scales = sbuf("w3_scales", [P, N], U8)
        interleave(nc.scalar.copy, w3_grouped, w3_raw)
        quantize(w3_words, w3_scales, w3_grouped[:].rearrange("p c j -> p (c j)"))

        for c, width in enumerate(STRETCHES):
            if c > 0:
                for t in slots:
                    add_control(t, c)
            hid_grouped = sbuf(f"hid_grouped{c}", [P, width, PACK], BF16)
            is_last = c == len(STRETCHES) - 1
            interleave(nc.vector.tensor_copy if is_last else nc.scalar.copy, hid_grouped, hid[c])
            hid_words = sbuf(f"hid_words{c}", [P, width], U32)
            hid_scales = sbuf(f"hid_scales{c}", [P, width], U8)
            quantize(hid_words, hid_scales, hid_grouped[:].rearrange("p c j -> p (c j)"))
            result = bank(PACK + c, f"result{c}", [P, width])
            nc.tensor.matmul_mx(
                out=result[:],
                lhsT=w3_words[:].bitcast(FP8X4),
                lhsT_scale=w3_scales[:],
                rhs=hid_words[:].bitcast(FP8X4),
                rhs_scale=hid_scales[:],
                start=True,
                stop=True,
            )
            staged = sbuf(f"staged{c}", [P, width], F32)
            nc.scalar.copy(staged[:], result[:])
            nc.sync.dma_start(out=out[:, starts[c] : starts[c] + width], in_=staged[:])
